import numpy as np
import ml_dtypes


def mxq(x, axis, fmt="e4m3"):
    dtype, down = {"e4m3": (ml_dtypes.float8_e4m3fn, 7), "e5m2": (ml_dtypes.float8_e5m2, 14)}[fmt]
    v = np.moveaxis(np.asarray(x, np.float32).astype(ml_dtypes.bfloat16).astype(np.float64), axis, -1)
    blocks = v.reshape(v.shape[:-1] + (-1, 32))
    amax = np.abs(blocks).max(-1, keepdims=True)
    byte = np.maximum(np.where(amax > 0, np.frexp(amax)[1] - 1 + 127, 0) - down, 1)
    scale = np.exp2(byte - 127.0)
    codes = (blocks / scale).astype(np.float32).astype(dtype).astype(np.float64)
    return np.moveaxis((codes * scale).reshape(v.shape), -1, axis)


WIDE = False


def mx_kscale(k):
    if not WIDE:
        return np.ones(k)
    levels = np.array([10, -10, 5, -5, 0])
    if k % 512:
        return np.exp2(np.random.permutation(np.resize(levels, k // 32))).repeat(32)
    a = np.empty((k // 512, 16))
    for p in range(k // 512):
        a[p, :8] = np.random.permutation(np.resize(levels, 8))
        for g in range(8):
            far = levels[np.abs(levels - a[p, g]) >= 10]
            a[p, g + 8] = far[np.random.randint(len(far))]
    return np.exp2(a.ravel()).repeat(32)


def f64(x):
    return np.asarray(x).astype(np.float64)


def striped(idx):
    return np.tile(idx.reshape(-1, 16).T, (8, 1)).astype(np.uint16)


def unstriped(offs):
    return offs[:16].T.reshape(-1).astype(np.int64)


K, T, E, C, N = 512, 2048, 16, 128, 128


def by_expert(wq, xq):
    return np.concatenate([wq[e].T @ xq[:, e * C:(e + 1) * C] for e in range(E)], axis=1)


def setup_inputs():
    n = np.random.standard_normal
    s = mx_kscale(K)[:, None]
    return {
        "xT": (n((K, T)) * s).astype(np.float32),
        "w": (n((E, K, N)) / np.sqrt(K) / s[None]).astype(np.float32),
        "offs": striped(np.random.permutation(T)[:E * C]),
    }


def reference(xT, w, offs):
    idx = unstriped(offs)
    xq = mxq(f64(xT)[:, idx], 0, "e4m3")
    y = by_expert(mxq(f64(w), 1, "e4m3"), xq)
    out = np.zeros((N, T))
    out[:, idx] = y
    return out

@@ -1,0 +1,146 @@
+from contextlib import ExitStack
+
+import concourse.mybir as mybir
+
+K, T, E, C, N = 512, 2048, 16, 128, 128
+FLOPS = 2 * K * N * E * C
+
+F32 = mybir.dt.float32
+BF16 = mybir.dt.bfloat16
+U32 = mybir.dt.uint32
+U16 = mybir.dt.uint16
+U8 = mybir.dt.uint8
+FP8X4 = mybir.dt.float8_e4m3fn_x4
+COPY = mybir.ActivationFunctionType.Copy
+MULT = mybir.AluOpType.mult
+ADD = mybir.AluOpType.add
+
+P = 128
+
+A_CHUNKS = (512, 512, 512, 256, 256)
+B_CHUNKS = (512, 512, 512, 512)
+VB = 1
+GS = 1024
+SS = 512
+WE = 2
+
+
+def tile_routed_moe_kernel(tc, xT, w, offs, out):
+    nc = tc.nc
+    with ExitStack() as ctx:
+        lists = ctx.enter_context(tc.tile_pool(name="lists", bufs=1))
+        keep = ctx.enter_context(tc.tile_pool(name="keep", bufs=1))
+        psum = ctx.enter_context(tc.psum_pool(name="psum", bufs=1))
+
+        offsets = lists.tile([P, E * C // 16], U16, name="offsets")
+        nc.sync.dma_start(offsets[:], offs)
+
+        warm_in = keep.tile([P, 1], F32, name="warm_in")
+        warm_out = keep.tile([P, 1], F32, name="warm_out")
+        nc.gpsimd.memset(warm_in[:], 0.0)
+        nc.scalar.copy(out=warm_out[:], in_=warm_in[:])
+
+        xv = xT.rearrange("(p u e) n -> p u e n", u=2, e=2)
+        raws = []
+        for u, chunks in enumerate((A_CHUNKS, B_CHUNKS)):
+            c0 = 0
+            for i, width in enumerate(chunks):
+                raw = keep.tile([P, 2, width], F32, name="raw%d_%d" % (u, i))
+                nc.sync.dma_start(out=raw[:], in_=xv[:, u, :, c0 : c0 + width])
+                raws.append((u, i, c0, width, raw))
+                c0 += width
+        wv = w.rearrange("e (p j) n -> p e j n", j=4)
+        wraws = []
+        for g in range(E // WE):
+            wraw = keep.tile([P, WE, 4, N], F32, name="wraw%d" % g)
+            nc.sync.dma_start(out=wraw[:], in_=wv[:, g * WE : (g + 1) * WE, :, :])
+            wraws.append(wraw)
+
+        wins = [keep.tile([P, T, 2], BF16, name="win%d" % u) for u in range(2)]
+        n_tiles = E * C // GS
+        halves = [keep.tile([P, 2, GS], U32, name="half%d" % i) for i in range(n_tiles)]
+
+        def round_chunk(engine_copy, u, c0, width, raw):
+            engine_copy(out=wins[u][:, c0 : c0 + width, :], in_=raw[:].rearrange("p e n -> p n e"))
+
+        def gather(u, i):
+            window = wins[u][:].rearrange("p n e -> p (n e)").bitcast(U32)
+            nc.vector.tensor_copy(
+                out=halves[i][:, u, :],
+                in_=window.indirect(offsets[:, i * GS // 16 : (i + 1) * GS // 16]),
+            )
+
+        for u, i, c0, width, raw in raws:
+            if u == 0:
+                round_chunk(nc.vector.tensor_copy, u, c0, width, raw)
+            elif i < len(B_CHUNKS) - VB:
+                round_chunk(nc.scalar.copy, u, c0, width, raw)
+        for i in range(n_tiles):
+            gather(0, i)
+        for u, i, c0, width, raw in raws:
+            if u == 1 and i >= len(B_CHUNKS) - VB:
+                round_chunk(nc.vector.tensor_copy, u, c0, width, raw)
+        for i in range(n_tiles):
+            gather(1, i)
+
+        xgs = []
+        for i in range(n_tiles):
+            xg = keep.tile([P, GS, 2, 2], BF16, name="xg%d" % i, align_bytes=64)
+            nc.vector.tensor_copy(
+                out=xg[:],
+                in_=halves[i][:].rearrange("p u n -> p (u n)").bitcast(BF16).rearrange("p (u n e) -> p n u e", u=2, e=2),
+            )
+            xgs.append(xg)
+
+        n_slices = E * C // SS
+        per = SS // C // WE
+        wgrs = [keep.tile([P, SS // C, N, 4], BF16, name="wgr%d" % s, align_bytes=64) for s in range(n_slices)]
+
+        def interleave_w(s):
+            for h in range(per):
+                nc.scalar.copy(
+                    out=wgrs[s][:, h * WE : (h + 1) * WE, :, :],
+                    in_=wraws[s * per + h][:].rearrange("p e j n -> p e n j"),
+                )
+
+        xcs = []
+        result = keep.tile([P, T], F32, name="result")
+        interleave_w(0)
+        for s in range(n_slices):
+            if s + 1 < n_slices:
+                interleave_w(s + 1)
+            if s * SS % GS == 0:
+                i = s * SS // GS
+                xc = keep.tile([P, GS], U32, name="xc%d" % i, align_bytes=64)
+                xs = keep.tile([P, GS], U8, name="xs%d" % i, align_bytes=64)
+                nc.vector.quantize_mx(
+                    out=xc[:].bitcast(FP8X4), scales=xs[:], in_=xgs[i][:].rearrange("p n u e -> p (n u e)")
+                )
+                xcs.append((xc, xs))
+            xc, xs = xcs[s * SS // GS]
+            x0 = s * SS % GS
+            wc = keep.tile([P, SS], U32, name="wc%d" % s, align_bytes=64)
+            ws = keep.tile([P, SS], U8, name="ws%d" % s, align_bytes=64)
+            nc.vector.quantize_mx(
+                out=wc[:].bitcast(FP8X4), scales=ws[:], in_=wgrs[s][:].rearrange("p e n j -> p (e n j)")
+            )
+            bank = psum.tile([P, SS], F32, name="bank%d" % s)
+            for i in range(SS // C):
+                cols = slice(i * C, (i + 1) * C)
+                xcols = slice(x0 + i * C, x0 + (i + 1) * C)
+                nc.tensor.matmul_mx(
+                    out=bank[:, cols],
+                    lhsT=wc[:, cols].bitcast(FP8X4),
+                    lhsT_scale=ws[:, cols],
+                    rhs=xc[:, xcols].bitcast(FP8X4),
+                    rhs_scale=xs[:, xcols],
+                    start=True,
+                    stop=True,
+                )
+            y = keep.tile([P, SS], F32, name="y%d" % s)
+            nc.scalar.copy(out=y[:], in_=bank[:])
+            nc.vector.tensor_copy(
+                out=result[:].indirect(offsets[:, s * SS // 16 : (s + 1) * SS // 16]), in_=y[:]
+            )
+
+        nc.sync.dma_start(out=out, in_=result[:])

@@ -18,8 +18,8 @@ ADD = mybir.AluOpType.add
 P = 128
 
 A_CHUNKS = (512, 512, 512, 256, 256)
-B_CHUNKS = (512, 512, 512, 512)
-VB = 1
+B_CHUNKS = (512, 512, 512, 256, 256)
+VB = 0
 GS = 1024
 SS = 512
 WE = 2
@@ -103,20 +103,19 @@ def tile_routed_moe_kernel(tc, xT, w, offs, out):
                     in_=wraws[s * per + h][:].rearrange("p e j n -> p e n j"),
                 )
 
-        xcs = []
         result = keep.tile([P, T], F32, name="result")
-        interleave_w(0)
-        for s in range(n_slices):
-            if s + 1 < n_slices:
-                interleave_w(s + 1)
-            if s * SS % GS == 0:
-                i = s * SS // GS
-                xc = keep.tile([P, GS], U32, name="xc%d" % i, align_bytes=64)
-                xs = keep.tile([P, GS], U8, name="xs%d" % i, align_bytes=64)
-                nc.vector.quantize_mx(
-                    out=xc[:].bitcast(FP8X4), scales=xs[:], in_=xgs[i][:].rearrange("p n u e -> p (n u e)")
-                )
-                xcs.append((xc, xs))
+        xcs = []
+        ys = []
+
+        def quantize_x(i):
+            xc = keep.tile([P, GS], U32, name="xc%d" % i, align_bytes=64)
+            xs = keep.tile([P, GS], U8, name="xs%d" % i, align_bytes=64)
+            nc.vector.quantize_mx(
+                out=xc[:].bitcast(FP8X4), scales=xs[:], in_=xgs[i][:].rearrange("p n u e -> p (n u e)")
+            )
+            xcs.append((xc, xs))
+
+        def multiply(s):
             xc, xs = xcs[s * SS // GS]
             x0 = s * SS % GS
             wc = keep.tile([P, SS], U32, name="wc%d" % s, align_bytes=64)
@@ -139,8 +138,24 @@ def tile_routed_moe_kernel(tc, xT, w, offs, out):
                 )
             y = keep.tile([P, SS], F32, name="y%d" % s)
             nc.scalar.copy(out=y[:], in_=bank[:])
+            ys.append(y)
+
+        def scatter(s):
             nc.vector.tensor_copy(
-                out=result[:].indirect(offsets[:, s * SS // 16 : (s + 1) * SS // 16]), in_=y[:]
+                out=result[:].indirect(offsets[:, s * SS // 16 : (s + 1) * SS // 16]), in_=ys[s][:]
             )
+
+        for s in range(n_slices):
+            interleave_w(s)
+        quantize_x(0)
+        multiply(0)
+        quantize_x(1)
+        multiply(1)
+        scatter(0)
+        multiply(2)
+        scatter(1)
+        multiply(3)
+        scatter(2)
+        scatter(3)
 
         nc.sync.dma_start(out=out, in_=result[:])

@@ -52,7 +52,7 @@ def tile_routed_moe_kernel(tc, xT, w, offs, out):
         wv = w.rearrange("e (p j) n -> p e j n", j=4)
         wraws = []
         for g in range(E // WE):
-            wraw = keep.tile([P, WE, 4, N], F32, name="wraw%d" % g)
+            wraw = keep.tile([P, WE, 4, N], F32, name="wraw%d" % g, tag="wraw%d" % g, align_bytes=64)
             nc.sync.dma_start(out=wraw[:], in_=wv[:, g * WE : (g + 1) * WE, :, :])
             wraws.append(wraw)
 
@@ -83,14 +83,15 @@ def tile_routed_moe_kernel(tc, xT, w, offs, out):
         for i in range(n_tiles):
             gather(1, i)
 
-        xgs = []
-        for i in range(n_tiles):
-            xg = keep.tile([P, GS, 2, 2], BF16, name="xg%d" % i, align_bytes=64)
-            nc.vector.tensor_copy(
-                out=xg[:],
-                in_=halves[i][:].rearrange("p u n -> p (u n)").bitcast(BF16).rearrange("p (u n e) -> p n u e", u=2, e=2),
-            )
-            xgs.append(xg)
+        xgs = {}
+
+        def interleave_x(engine_copy, s0, n_slots, tag):
+            xg = keep.tile([P, n_slots, 2, 2], BF16, name="xg%d" % s0, tag=tag, align_bytes=64)
+            words = halves[s0 // GS][:, :, s0 % GS : s0 % GS + n_slots]
+            engine_copy(out=xg[:], in_=words.bitcast(BF16).rearrange("p u (n e) -> p n u e", e=2))
+            xgs[s0] = xg
+
+        interleave_x(nc.vector.tensor_copy, 0, GS, "xg0")
 
         n_slices = E * C // SS
         per = SS // C // WE
@@ -107,17 +108,17 @@ def tile_routed_moe_kernel(tc, xT, w, offs, out):
         xcs = []
         ys = []
 
-        def quantize_x(i):
-            xc = keep.tile([P, GS], U32, name="xc%d" % i, align_bytes=64)
-            xs = keep.tile([P, GS], U8, name="xs%d" % i, align_bytes=64)
+        def quantize_x(s0, n_slots):
+            xc = keep.tile([P, n_slots], U32, name="xc%d" % s0, align_bytes=64)
+            xs = keep.tile([P, n_slots], U8, name="xs%d" % s0, align_bytes=64)
             nc.vector.quantize_mx(
-                out=xc[:].bitcast(FP8X4), scales=xs[:], in_=xgs[i][:].rearrange("p n u e -> p (n u e)")
+                out=xc[:].bitcast(FP8X4), scales=xs[:], in_=xgs[s0][:].rearrange("p n u e -> p (n u e)")
             )
-            xcs.append((xc, xs))
+            for s in range(s0 // SS, (s0 + n_slots) // SS):
+                xcs.append((xc, xs, s * SS - s0))
 
-        def multiply(s):
-            xc, xs = xcs[s * SS // GS]
-            x0 = s * SS % GS
+        def multiply(s, scale=None, y_tag=None):
+            xc, xs, x0 = xcs[s]
             wc = keep.tile([P, SS], U32, name="wc%d" % s, align_bytes=64)
             ws = keep.tile([P, SS], U8, name="ws%d" % s, align_bytes=64)
             nc.vector.quantize_mx(
@@ -136,8 +137,11 @@ def tile_routed_moe_kernel(tc, xT, w, offs, out):
                     start=True,
                     stop=True,
                 )
-            y = keep.tile([P, SS], F32, name="y%d" % s)
-            nc.scalar.copy(out=y[:], in_=bank[:])
+            y = keep.tile([P, SS], F32, name="y%d" % s, tag=y_tag or "y%d" % s, align_bytes=64)
+            if scale is None:
+                nc.scalar.copy(out=y[:], in_=bank[:])
+            else:
+                nc.scalar.activation(out=y[:], in_=bank[:], func=COPY, scale=scale[:, 0:1])
             ys.append(y)
 
         def scatter(s):
@@ -147,13 +151,27 @@ def tile_routed_moe_kernel(tc, xT, w, offs, out):
 
         for s in range(n_slices):
             interleave_w(s)
-        quantize_x(0)
-        multiply(0)
-        quantize_x(1)
-        multiply(1)
+        quantize_x(0, GS)
+        def ones_on(tag):
+            one = keep.tile([P, 1], F32, name="one_" + tag, tag=tag, align_bytes=64)
+            nc.gpsimd.memset(one[:], 1.0)
+            return one
+
+        def scaled_copy(one):
+            return lambda out, in_: nc.scalar.activation(out=out, in_=in_, func=COPY, scale=one[:, 0:1])
+
+        one_a = ones_on("wraw7")
+        one_b = ones_on("wraw6")
+        one_c = ones_on("wraw5")
+        multiply(0, scale=one_a)
+        interleave_x(scaled_copy(one_b), GS, SS, "wraw7")
+        multiply(1, scale=one_c, y_tag="wraw6")
+        interleave_x(nc.scalar.copy, GS + SS, SS, "wraw5")
         scatter(0)
+        quantize_x(GS, SS)
         multiply(2)
         scatter(1)
+        quantize_x(GS + SS, SS)
         multiply(3)
         scatter(2)
         scatter(3)

@@ -100,8 +100,8 @@ def tile_routed_moe_kernel(tc, xT, w, offs, out):
         def interleave_w(s):
             for h in range(per):
                 nc.scalar.copy(
-                    out=wgrs[s][:, h * WE : (h + 1) * WE, :, :],
-                    in_=wraws[s * per + h][:].rearrange("p e j n -> p e n j"),
+                    out=wgrs[s][:, h * WE : (h + 1) * WE, :, :].rearrange("p e (c i) j -> p e c j i", i=4),
+                    in_=wraws[s * per + h][:].rearrange("p e j (c i) -> p e c j i", i=4),
                 )
 
         result = keep.tile([P, T], F32, name="result")

@@ -39,6 +39,10 @@ def tile_routed_moe_kernel(tc, xT, w, offs, out):
         warm_out = keep.tile([P, 1], F32, name="warm_out")
         nc.gpsimd.memset(warm_in[:], 0.0)
         nc.scalar.copy(out=warm_out[:], in_=warm_in[:])
+        ones = {}
+        for tag in ("fence_a", "fence_b", "fence_c"):
+            ones[tag] = keep.tile([P, 1], F32, name="one_" + tag, tag=tag, align_bytes=64)
+            nc.gpsimd.memset(ones[tag][:], 1.0)
 
         xv = xT.rearrange("(p u e) n -> p u e n", u=2, e=2)
         raws = []
@@ -152,21 +156,13 @@ def tile_routed_moe_kernel(tc, xT, w, offs, out):
         for s in range(n_slices):
             interleave_w(s)
         quantize_x(0, GS)
-        def ones_on(tag):
-            one = keep.tile([P, 1], F32, name="one_" + tag, tag=tag, align_bytes=64)
-            nc.gpsimd.memset(one[:], 1.0)
-            return one
-
         def scaled_copy(one):
             return lambda out, in_: nc.scalar.activation(out=out, in_=in_, func=COPY, scale=one[:, 0:1])
 
-        one_a = ones_on("wraw7")
-        one_b = ones_on("wraw6")
-        one_c = ones_on("wraw5")
-        multiply(0, scale=one_a)
-        interleave_x(scaled_copy(one_b), GS, SS, "wraw7")
-        multiply(1, scale=one_c, y_tag="wraw6")
-        interleave_x(nc.scalar.copy, GS + SS, SS, "wraw5")
+        multiply(0, scale=ones["fence_a"], y_tag="wraw7")
+        interleave_x(scaled_copy(ones["fence_b"]), GS, SS, "fence_a")
+        multiply(1, scale=ones["fence_c"], y_tag="fence_b")
+        interleave_x(nc.scalar.copy, GS + SS, SS, "fence_c")
         scatter(0)
         quantize_x(GS, SS)
         multiply(2)

@@ -40,7 +40,7 @@ def tile_routed_moe_kernel(tc, xT, w, offs, out):
         nc.gpsimd.memset(warm_in[:], 0.0)
         nc.scalar.copy(out=warm_out[:], in_=warm_in[:])
         ones = {}
-        for tag in ("fence_a", "fence_b", "fence_c"):
+        for tag in ("fence_a", "fence_c"):
             ones[tag] = keep.tile([P, 1], F32, name="one_" + tag, tag=tag, align_bytes=64)
             nc.gpsimd.memset(ones[tag][:], 1.0)
 
@@ -61,17 +61,19 @@ def tile_routed_moe_kernel(tc, xT, w, offs, out):
             wraws.append(wraw)
 
         wins = [keep.tile([P, T, 2], BF16, name="win%d" % u) for u in range(2)]
-        n_tiles = E * C // GS
-        halves = [keep.tile([P, 2, GS], U32, name="half%d" % i) for i in range(n_tiles)]
+        PIECES = ((0, GS), (GS, SS), (GS + SS, SS))
+        halves = {}
+        for s0, n_slots in PIECES:
+            halves[s0] = keep.tile([P, 2, n_slots], U32, name="half%d" % s0, tag="half%d" % s0, align_bytes=64)
 
         def round_chunk(engine_copy, u, c0, width, raw):
             engine_copy(out=wins[u][:, c0 : c0 + width, :], in_=raw[:].rearrange("p e n -> p n e"))
 
-        def gather(u, i):
+        def gather(u, s0, n_slots):
             window = wins[u][:].rearrange("p n e -> p (n e)").bitcast(U32)
             nc.vector.tensor_copy(
-                out=halves[i][:, u, :],
-                in_=window.indirect(offsets[:, i * GS // 16 : (i + 1) * GS // 16]),
+                out=halves[s0][:, u, :],
+                in_=window.indirect(offsets[:, s0 // 16 : (s0 + n_slots) // 16]),
             )
 
         for u, i, c0, width, raw in raws:
@@ -79,20 +81,26 @@ def tile_routed_moe_kernel(tc, xT, w, offs, out):
                 round_chunk(nc.vector.tensor_copy, u, c0, width, raw)
             elif i < len(B_CHUNKS) - VB:
                 round_chunk(nc.scalar.copy, u, c0, width, raw)
-        for i in range(n_tiles):
-            gather(0, i)
+        for s0, n_slots in PIECES:
+            gather(0, s0, n_slots)
         for u, i, c0, width, raw in raws:
             if u == 1 and i >= len(B_CHUNKS) - VB:
                 round_chunk(nc.vector.tensor_copy, u, c0, width, raw)
-        for i in range(n_tiles):
-            gather(1, i)
+        for s0, n_slots in PIECES:
+            gather(1, s0, n_slots)
 
         xgs = {}
 
-        def interleave_x(engine_copy, s0, n_slots, tag):
+        def interleave_x(engine_copy, s0, n_slots, tag, run=1):
             xg = keep.tile([P, n_slots, 2, 2], BF16, name="xg%d" % s0, tag=tag, align_bytes=64)
-            words = halves[s0 // GS][:, :, s0 % GS : s0 % GS + n_slots]
-            engine_copy(out=xg[:], in_=words.bitcast(BF16).rearrange("p u (n e) -> p n u e", e=2))
+            values = halves[s0][:].rearrange("p u n -> p (u n)").bitcast(BF16)
+            if run == 1:
+                engine_copy(out=xg[:], in_=values.rearrange("p (u n e) -> p n u e", u=2, e=2))
+            else:
+                engine_copy(
+                    out=xg[:].rearrange("p (c i) u e -> p c u i e", i=run),
+                    in_=values.rearrange("p (u c i e) -> p c u i e", u=2, i=run, e=2),
+                )
             xgs[s0] = xg
 
         interleave_x(nc.vector.tensor_copy, 0, GS, "xg0")
@@ -156,13 +164,10 @@ def tile_routed_moe_kernel(tc, xT, w, offs, out):
         for s in range(n_slices):
             interleave_w(s)
         quantize_x(0, GS)
-        def scaled_copy(one):
-            return lambda out, in_: nc.scalar.activation(out=out, in_=in_, func=COPY, scale=one[:, 0:1])
-
         multiply(0, scale=ones["fence_a"], y_tag="wraw7")
-        interleave_x(scaled_copy(ones["fence_b"]), GS, SS, "fence_a")
-        multiply(1, scale=ones["fence_c"], y_tag="fence_b")
-        interleave_x(nc.scalar.copy, GS + SS, SS, "fence_c")
+        interleave_x(nc.scalar.copy, GS, SS, "fence_a", run=4)
+        multiply(1, scale=ones["fence_c"], y_tag="half%d" % GS)
+        interleave_x(nc.scalar.copy, GS + SS, SS, "fence_c", run=4)
         scatter(0)
         quantize_x(GS, SS)
         multiply(2)

@@ -91,16 +91,13 @@ def tile_routed_moe_kernel(tc, xT, w, offs, out):
 
         xgs = {}
 
-        def interleave_x(engine_copy, s0, n_slots, tag, run=1):
+        def interleave_x(engine_copy, s0, n_slots, tag, run=4):
             xg = keep.tile([P, n_slots, 2, 2], BF16, name="xg%d" % s0, tag=tag, align_bytes=64)
             values = halves[s0][:].rearrange("p u n -> p (u n)").bitcast(BF16)
-            if run == 1:
-                engine_copy(out=xg[:], in_=values.rearrange("p (u n e) -> p n u e", u=2, e=2))
-            else:
-                engine_copy(
-                    out=xg[:].rearrange("p (c i) u e -> p c u i e", i=run),
-                    in_=values.rearrange("p (u c i e) -> p c u i e", u=2, i=run, e=2),
-                )
+            engine_copy(
+                out=xg[:].rearrange("p (c i) u e -> p c u i e", i=run),
+                in_=values.rearrange("p (u c i e) -> p c u i e", u=2, i=run, e=2),
+            )
             xgs[s0] = xg
 
         interleave_x(nc.vector.tensor_copy, 0, GS, "xg0")

@@ -17,7 +17,7 @@ ADD = mybir.AluOpType.add
 
 P = 128
 
-A_CHUNKS = (512, 512, 512, 256, 256)
+A_CHUNKS = (1280, 512, 256)
 B_CHUNKS = (512, 512, 512, 256, 256)
 VB = 0
 GS = 1024
@@ -33,7 +33,6 @@ def tile_routed_moe_kernel(tc, xT, w, offs, out):
         psum = ctx.enter_context(tc.psum_pool(name="psum", bufs=1))
 
         offsets = lists.tile([P, E * C // 16], U16, name="offsets")
-        nc.sync.dma_start(offsets[:], offs)
 
         warm_in = keep.tile([P, 1], F32, name="warm_in")
         warm_out = keep.tile([P, 1], F32, name="warm_out")
@@ -53,6 +52,8 @@ def tile_routed_moe_kernel(tc, xT, w, offs, out):
                 nc.sync.dma_start(out=raw[:], in_=xv[:, u, :, c0 : c0 + width])
                 raws.append((u, i, c0, width, raw))
                 c0 += width
+            if u == 0:
+                nc.sync.dma_start(offsets[:], offs)
         wv = w.rearrange("e (p j) n -> p e j n", j=4)
         wraws = []
         for g in range(E // WE):

@@ -17,8 +17,8 @@ ADD = mybir.AluOpType.add
 
 P = 128
 
-A_CHUNKS = (1280, 512, 256)
-B_CHUNKS = (512, 512, 512, 256, 256)
+A_CHUNKS = (1024, 640, 256, 128)
+B_CHUNKS = (256,) * 8
 VB = 0
 GS = 1024
 SS = 512

@@ -11,16 +11,13 @@ U32 = mybir.dt.uint32
 U16 = mybir.dt.uint16
 U8 = mybir.dt.uint8
 FP8X4 = mybir.dt.float8_e4m3fn_x4
+
 COPY = mybir.ActivationFunctionType.Copy
-MULT = mybir.AluOpType.mult
-ADD = mybir.AluOpType.add
 
 P = 128
 
 A_CHUNKS = (1024, 640, 256, 128)
 B_CHUNKS = (256,) * 8
-VB = 0
-GS = 1024
 SS = 512
 WE = 2
 
@@ -38,10 +35,12 @@ def tile_routed_moe_kernel(tc, xT, w, offs, out):
         warm_out = keep.tile([P, 1], F32, name="warm_out")
         nc.gpsimd.memset(warm_in[:], 0.0)
         nc.scalar.copy(out=warm_out[:], in_=warm_in[:])
-        ones = {}
-        for tag in ("fence_a", "fence_c"):
-            ones[tag] = keep.tile([P, 1], F32, name="one_" + tag, tag=tag, align_bytes=64)
-            nc.gpsimd.memset(ones[tag][:], 1.0)
+
+        ones = []
+        for s in range(2):
+            one = keep.tile([P, 1], F32, name="one%d" % s, tag="behind%d" % s, align_bytes=64)
+            nc.gpsimd.memset(one[:], 1.0)
+            ones.append(one)
 
         xv = xT.rearrange("(p u e) n -> p u e n", u=2, e=2)
         raws = []
@@ -62,96 +61,92 @@ def tile_routed_moe_kernel(tc, xT, w, offs, out):
             wraws.append(wraw)
 
         wins = [keep.tile([P, T, 2], BF16, name="win%d" % u) for u in range(2)]
-        PIECES = ((0, GS), (GS, SS), (GS + SS, SS))
-        halves = {}
-        for s0, n_slots in PIECES:
-            halves[s0] = keep.tile([P, 2, n_slots], U32, name="half%d" % s0, tag="half%d" % s0, align_bytes=64)
+        n_slices = E * C // SS
+        halves = [
+            keep.tile([P, 2, SS], U32, name="half%d" % s, tag="half%d" % s, align_bytes=64) for s in range(n_slices)
+        ]
 
-        def round_chunk(engine_copy, u, c0, width, raw):
+        for u, i, c0, width, raw in raws:
+            engine_copy = nc.vector.tensor_copy if u == 0 else nc.scalar.copy
             engine_copy(out=wins[u][:, c0 : c0 + width, :], in_=raw[:].rearrange("p e n -> p n e"))
 
-        def gather(u, s0, n_slots):
+        def gather(u, s):
             window = wins[u][:].rearrange("p n e -> p (n e)").bitcast(U32)
             nc.vector.tensor_copy(
-                out=halves[s0][:, u, :],
-                in_=window.indirect(offsets[:, s0 // 16 : (s0 + n_slots) // 16]),
+                out=halves[s][:, u, :],
+                in_=window.indirect(offsets[:, s * SS // 16 : (s + 1) * SS // 16]),
             )
 
-        for u, i, c0, width, raw in raws:
-            if u == 0:
-                round_chunk(nc.vector.tensor_copy, u, c0, width, raw)
-            elif i < len(B_CHUNKS) - VB:
-                round_chunk(nc.scalar.copy, u, c0, width, raw)
-        for s0, n_slots in PIECES:
-            gather(0, s0, n_slots)
-        for u, i, c0, width, raw in raws:
-            if u == 1 and i >= len(B_CHUNKS) - VB:
-                round_chunk(nc.vector.tensor_copy, u, c0, width, raw)
-        for s0, n_slots in PIECES:
-            gather(1, s0, n_slots)
+        for s in range(n_slices):
+            gather(0, s)
+        for s in range(n_slices - 1):
+            gather(1, s)
 
-        xgs = {}
-
-        def interleave_x(engine_copy, s0, n_slots, tag, run=4):
-            xg = keep.tile([P, n_slots, 2, 2], BF16, name="xg%d" % s0, tag=tag, align_bytes=64)
-            values = halves[s0][:].rearrange("p u n -> p (u n)").bitcast(BF16)
-            engine_copy(
-                out=xg[:].rearrange("p (c i) u e -> p c u i e", i=run),
-                in_=values.rearrange("p (u c i e) -> p c u i e", u=2, i=run, e=2),
-            )
-            xgs[s0] = xg
-
-        interleave_x(nc.vector.tensor_copy, 0, GS, "xg0")
-
-        n_slices = E * C // SS
         per = SS // C // WE
-        wgrs = [keep.tile([P, SS // C, N, 4], BF16, name="wgr%d" % s, align_bytes=64) for s in range(n_slices)]
+        wgrs = []
 
-        def interleave_w(s):
-            for h in range(per):
-                nc.scalar.copy(
-                    out=wgrs[s][:, h * WE : (h + 1) * WE, :, :].rearrange("p e (c i) j -> p e c j i", i=4),
-                    in_=wraws[s * per + h][:].rearrange("p e j (c i) -> p e c j i", i=4),
-                )
+        def new_weights(s, tag):
+            wgr = keep.tile([P, SS // C, N, 4], BF16, name="wgr%d" % s, tag=tag, align_bytes=64)
+            wgrs.append(wgr)
+
+        def interleave_w(g):
+            e0 = (g % per) * WE
+            nc.scalar.copy(
+                out=wgrs[g // per][:, e0 : e0 + WE, :, :].rearrange("p e (c i) j -> p e c j i", i=4),
+                in_=wraws[g][:].rearrange("p e j (c i) -> p e c j i", i=4),
+            )
+
+        xgs = []
+
+        def interleave_x(s, tag):
+            xg = keep.tile([P, SS, 2], U32, name="xg%d" % s, tag=tag, align_bytes=64)
+            nc.scalar.copy(
+                out=xg[:].rearrange("p (c i) u -> p c u i", i=4),
+                in_=halves[s][:].rearrange("p u (c i) -> p c u i", i=4),
+            )
+            xgs.append(xg)
+
+        def quantize(name, in_):
+            codes = keep.tile([P, SS], U32, name=name + "_codes", align_bytes=64)
+            scales = keep.tile([P, SS], U8, name=name + "_scales", align_bytes=64)
+            nc.vector.quantize_mx(out=codes[:].bitcast(FP8X4), scales=scales[:], in_=in_)
+            return codes, scales
 
         result = keep.tile([P, T], F32, name="result")
-        xcs = []
+        xqs = []
+        wqs = []
+        banks = []
         ys = []
 
-        def quantize_x(s0, n_slots):
-            xc = keep.tile([P, n_slots], U32, name="xc%d" % s0, align_bytes=64)
-            xs = keep.tile([P, n_slots], U8, name="xs%d" % s0, align_bytes=64)
-            nc.vector.quantize_mx(
-                out=xc[:].bitcast(FP8X4), scales=xs[:], in_=xgs[s0][:].rearrange("p n u e -> p (n u e)")
-            )
-            for s in range(s0 // SS, (s0 + n_slots) // SS):
-                xcs.append((xc, xs, s * SS - s0))
+        def quantize_x(s):
+            xqs.append(quantize("x%d" % s, xgs[s][:].rearrange("p n u -> p (n u)").bitcast(BF16)))
 
-        def multiply(s, scale=None, y_tag=None):
-            xc, xs, x0 = xcs[s]
-            wc = keep.tile([P, SS], U32, name="wc%d" % s, align_bytes=64)
-            ws = keep.tile([P, SS], U8, name="ws%d" % s, align_bytes=64)
-            nc.vector.quantize_mx(
-                out=wc[:].bitcast(FP8X4), scales=ws[:], in_=wgrs[s][:].rearrange("p e n j -> p (e n j)")
-            )
+        def quantize_w(s):
+            wqs.append(quantize("w%d" % s, wgrs[s][:].rearrange("p e n j -> p (e n j)")))
+
+        def multiply(s):
+            xc, xs = xqs[s]
+            wc, ws = wqs[s]
             bank = psum.tile([P, SS], F32, name="bank%d" % s)
             for i in range(SS // C):
                 cols = slice(i * C, (i + 1) * C)
-                xcols = slice(x0 + i * C, x0 + (i + 1) * C)
                 nc.tensor.matmul_mx(
                     out=bank[:, cols],
                     lhsT=wc[:, cols].bitcast(FP8X4),
                     lhsT_scale=ws[:, cols],
-                    rhs=xc[:, xcols].bitcast(FP8X4),
-                    rhs_scale=xs[:, xcols],
+                    rhs=xc[:, cols].bitcast(FP8X4),
+                    rhs_scale=xs[:, cols],
                     start=True,
                     stop=True,
                 )
-            y = keep.tile([P, SS], F32, name="y%d" % s, tag=y_tag or "y%d" % s, align_bytes=64)
-            if scale is None:
-                nc.scalar.copy(out=y[:], in_=bank[:])
+            banks.append(bank)
+
+        def take_out(s, tag):
+            y = keep.tile([P, SS], F32, name="y%d" % s, tag=tag, align_bytes=64)
+            if s < 2:
+                nc.scalar.activation(out=y[:], in_=banks[s][:], func=COPY, scale=ones[s][:, 0:1])
             else:
-                nc.scalar.activation(out=y[:], in_=bank[:], func=COPY, scale=scale[:, 0:1])
+                nc.scalar.copy(out=y[:], in_=banks[s][:])
             ys.append(y)
 
         def scatter(s):
@@ -159,20 +154,42 @@ def tile_routed_moe_kernel(tc, xT, w, offs, out):
                 out=result[:].indirect(offsets[:, s * SS // 16 : (s + 1) * SS // 16]), in_=ys[s][:]
             )
 
-        for s in range(n_slices):
-            interleave_w(s)
-        quantize_x(0, GS)
-        multiply(0, scale=ones["fence_a"], y_tag="wraw7")
-        interleave_x(nc.scalar.copy, GS, SS, "fence_a", run=4)
-        multiply(1, scale=ones["fence_c"], y_tag="half%d" % GS)
-        interleave_x(nc.scalar.copy, GS + SS, SS, "fence_c", run=4)
+        new_weights(0, "wgr0")
+        new_weights(1, "wgr1")
+        interleave_w(0)
+        interleave_x(0, "wraw0")
+        interleave_w(1)
+        interleave_x(1, "wraw1")
+        interleave_w(2)
+        interleave_w(3)
+        quantize_w(0)
+        quantize_x(0)
+        multiply(0)
+        gather(1, 3)
+        quantize_x(1)
+        quantize_w(1)
+        multiply(1)
+        take_out(0, "wraw3")
         scatter(0)
-        quantize_x(GS, SS)
+        new_weights(2, "behind0")
+        interleave_w(4)
+        interleave_w(5)
+        interleave_x(2, "wraw5")
+        take_out(1, "half2")
+        quantize_w(2)
+        quantize_x(2)
         multiply(2)
         scatter(1)
-        quantize_x(GS + SS, SS)
+        new_weights(3, "behind1")
+        interleave_w(6)
+        interleave_w(7)
+        interleave_x(3, "wraw7")
+        take_out(2, "half3")
+        quantize_w(3)
+        quantize_x(3)
         multiply(3)
         scatter(2)
+        take_out(3, "y3")
         scatter(3)
 
         nc.sync.dma_start(out=out, in_=result[:])

@@ -83,50 +83,31 @@ def tile_routed_moe_kernel(tc, xT, w, offs, out):
             gather(1, s)
 
         per = SS // C // WE
-        wgrs = []
 
-        def new_weights(s, tag):
-            wgr = keep.tile([P, SS // C, N, 4], BF16, name="wgr%d" % s, tag=tag, align_bytes=64)
-            wgrs.append(wgr)
-
-        def interleave_w(g):
+        def interleave_w(g, wg):
             e0 = (g % per) * WE
             nc.scalar.copy(
-                out=wgrs[g // per][:, e0 : e0 + WE, :, :].rearrange("p e (c i) j -> p e c j i", i=4),
+                out=wg[:, e0 : e0 + WE, :, :].rearrange("p e (c i) j -> p e c j i", i=4),
                 in_=wraws[g][:].rearrange("p e j (c i) -> p e c j i", i=4),
             )
 
-        xgs = []
-
-        def interleave_x(s, tag):
-            xg = keep.tile([P, SS, 2], U32, name="xg%d" % s, tag=tag, align_bytes=64)
-            nc.scalar.copy(
-                out=xg[:].rearrange("p (c i) u -> p c u i", i=4),
-                in_=halves[s][:].rearrange("p u (c i) -> p c u i", i=4),
-            )
-            xgs.append(xg)
+        def interleave_x(s, xg):
+            nc.scalar.copy(out=xg, in_=halves[s][:].rearrange("p u n -> p n u"))
 
         def quantize(name, in_):
-            codes = keep.tile([P, SS], U32, name=name + "_codes", align_bytes=64)
-            scales = keep.tile([P, SS], U8, name=name + "_scales", align_bytes=64)
+            columns = in_.shape[1] // 4
+            codes = keep.tile([P, columns], U32, name=name + "_codes", align_bytes=64)
+            scales = keep.tile([P, columns], U8, name=name + "_scales", align_bytes=64)
             nc.vector.quantize_mx(out=codes[:].bitcast(FP8X4), scales=scales[:], in_=in_)
-            return codes, scales
+            return [(codes[:, c0 : c0 + SS], scales[:, c0 : c0 + SS]) for c0 in range(0, columns, SS)]
 
         result = keep.tile([P, T], F32, name="result")
-        xqs = []
-        wqs = []
         banks = []
         ys = []
 
-        def quantize_x(s):
-            xqs.append(quantize("x%d" % s, xgs[s][:].rearrange("p n u -> p (n u)").bitcast(BF16)))
-
-        def quantize_w(s):
-            wqs.append(quantize("w%d" % s, wgrs[s][:].rearrange("p e n j -> p (e n j)")))
-
-        def multiply(s):
-            xc, xs = xqs[s]
-            wc, ws = wqs[s]
+        def multiply(s, weights, slots):
+            wc, ws = weights
+            xc, xs = slots
             bank = psum.tile([P, SS], F32, name="bank%d" % s)
             for i in range(SS // C):
                 cols = slice(i * C, (i + 1) * C)
@@ -154,42 +135,32 @@ def tile_routed_moe_kernel(tc, xT, w, offs, out):
                 out=result[:].indirect(offsets[:, s * SS // 16 : (s + 1) * SS // 16]), in_=ys[s][:]
             )
 
-        new_weights(0, "wgr0")
-        new_weights(1, "wgr1")
-        interleave_w(0)
-        interleave_x(0, "wraw0")
-        interleave_w(1)
-        interleave_x(1, "wraw1")
-        interleave_w(2)
-        interleave_w(3)
-        quantize_w(0)
-        quantize_x(0)
-        multiply(0)
-        gather(1, 3)
-        quantize_x(1)
-        quantize_w(1)
-        multiply(1)
-        take_out(0, "wraw3")
-        scatter(0)
-        new_weights(2, "behind0")
-        interleave_w(4)
-        interleave_w(5)
-        interleave_x(2, "wraw5")
-        take_out(1, "half2")
-        quantize_w(2)
-        quantize_x(2)
-        multiply(2)
-        scatter(1)
-        new_weights(3, "behind1")
-        interleave_w(6)
-        interleave_w(7)
-        interleave_x(3, "wraw7")
-        take_out(2, "half3")
-        quantize_w(3)
-        quantize_x(3)
-        multiply(3)
-        scatter(2)
-        take_out(3, "y3")
-        scatter(3)
+        wgs = [keep.tile([P, SS // C, N, 4], BF16, name="wg%d" % s, align_bytes=64) for s in range(2)]
+        xgs = []
+        for s in range(2):
+            interleave_w(s, wgs[0])
+            xg = keep.tile([P, SS, 2], U32, name="xg%d" % s, tag="wraw%d" % s, align_bytes=64)
+            interleave_x(s, xg[:])
+            xgs.append(xg)
+        for g in range(2, 4):
+            interleave_w(g, wgs[1])
+        for s in range(2):
+            weights = quantize("w%d" % s, wgs[s][:].rearrange("p e n j -> p (e n j)"))[0]
+            slots = quantize("x%d" % s, xgs[s][:].rearrange("p n u -> p (n u)").bitcast(BF16))[0]
+            multiply(s, weights, slots)
+            if s == 0:
+                gather(1, 3)
+        for s in range(2, n_slices):
+            take_out(s - 2, "wraw%d" % (2 * s - 1))
+            scatter(s - 2)
+            both = keep.tile([P, 2, 4 * SS], BF16, name="both%d" % s, tag="behind%d" % (s - 2), align_bytes=64)
+            interleave_x(s, both[:, 1, :].bitcast(U32).rearrange("p (n u) -> p n u", u=2))
+            wg = both[:, 0, :].rearrange("p (e n j) -> p e n j", n=N, j=4)
+            for g in range(s * per, (s + 1) * per):
+                interleave_w(g, wg)
+            multiply(s, *quantize("both%d" % s, both[:].rearrange("p h c -> p (h c)")))
+        for s in range(2, n_slices):
+            take_out(s, "y%d" % s)
+            scatter(s)
 
         nc.sync.dma_start(out=out, in_=result[:])

from contextlib import ExitStack

import concourse.mybir as mybir

K, T, E, C, N = 512, 2048, 16, 128, 128
FLOPS = 2 * K * N * E * C

F32 = mybir.dt.float32
BF16 = mybir.dt.bfloat16
U32 = mybir.dt.uint32
U16 = mybir.dt.uint16
U8 = mybir.dt.uint8
FP8X4 = mybir.dt.float8_e4m3fn_x4

COPY = mybir.ActivationFunctionType.Copy

P = 128

A_CHUNKS = (1024, 640, 256, 128)
B_CHUNKS = (256,) * 8
SS = 512
WE = 2


def tile_routed_moe_kernel(tc, xT, w, offs, out):
    nc = tc.nc
    with ExitStack() as ctx:
        lists = ctx.enter_context(tc.tile_pool(name="lists", bufs=1))
        keep = ctx.enter_context(tc.tile_pool(name="keep", bufs=1))
        psum = ctx.enter_context(tc.psum_pool(name="psum", bufs=1))

        offsets = lists.tile([P, E * C // 16], U16, name="offsets")

        warm_in = keep.tile([P, 1], F32, name="warm_in")
        warm_out = keep.tile([P, 1], F32, name="warm_out")
        nc.gpsimd.memset(warm_in[:], 0.0)
        nc.scalar.copy(out=warm_out[:], in_=warm_in[:])

        ones = []
        for s in range(2):
            one = keep.tile([P, 1], F32, name="one%d" % s, tag="behind%d" % s, align_bytes=64)
            nc.gpsimd.memset(one[:], 1.0)
            ones.append(one)

        xv = xT.rearrange("(p u e) n -> p u e n", u=2, e=2)
        raws = []
        for u, chunks in enumerate((A_CHUNKS, B_CHUNKS)):
            c0 = 0
            for i, width in enumerate(chunks):
                raw = keep.tile([P, 2, width], F32, name="raw%d_%d" % (u, i))
                nc.sync.dma_start(out=raw[:], in_=xv[:, u, :, c0 : c0 + width])
                raws.append((u, i, c0, width, raw))
                c0 += width
            if u == 0:
                nc.sync.dma_start(offsets[:], offs)
        wv = w.rearrange("e (p j) n -> p e j n", j=4)
        wraws = []
        for g in range(E // WE):
            wraw = keep.tile([P, WE, 4, N], F32, name="wraw%d" % g, tag="wraw%d" % g, align_bytes=64)
            nc.sync.dma_start(out=wraw[:], in_=wv[:, g * WE : (g + 1) * WE, :, :])
            wraws.append(wraw)

        wins = [keep.tile([P, T, 2], BF16, name="win%d" % u) for u in range(2)]
        n_slices = E * C // SS
        halves = [
            keep.tile([P, 2, SS], U32, name="half%d" % s, tag="half%d" % s, align_bytes=64) for s in range(n_slices)
        ]

        for u, i, c0, width, raw in raws:
            engine_copy = nc.vector.tensor_copy if u == 0 else nc.scalar.copy
            engine_copy(out=wins[u][:, c0 : c0 + width, :], in_=raw[:].rearrange("p e n -> p n e"))

        def gather(u, s):
            window = wins[u][:].rearrange("p n e -> p (n e)").bitcast(U32)
            nc.vector.tensor_copy(
                out=halves[s][:, u, :],
                in_=window.indirect(offsets[:, s * SS // 16 : (s + 1) * SS // 16]),
            )

        for s in range(n_slices):
            gather(0, s)
        for s in range(n_slices - 1):
            gather(1, s)

        per = SS // C // WE

        def interleave_w(g, wg):
            e0 = (g % per) * WE
            nc.scalar.copy(
                out=wg[:, e0 : e0 + WE, :, :].rearrange("p e (c i) j -> p e c j i", i=4),
                in_=wraws[g][:].rearrange("p e j (c i) -> p e c j i", i=4),
            )

        def interleave_x(s, xg):
            nc.scalar.copy(out=xg, in_=halves[s][:].rearrange("p u n -> p n u"))

        def quantize(name, in_):
            columns = in_.shape[1] // 4
            codes = keep.tile([P, columns], U32, name=name + "_codes", align_bytes=64)
            scales = keep.tile([P, columns], U8, name=name + "_scales", align_bytes=64)
            nc.vector.quantize_mx(out=codes[:].bitcast(FP8X4), scales=scales[:], in_=in_)
            return [(codes[:, c0 : c0 + SS], scales[:, c0 : c0 + SS]) for c0 in range(0, columns, SS)]

        result = keep.tile([P, T], F32, name="result")
        banks = []
        ys = []

        def multiply(s, weights, slots):
            wc, ws = weights
            xc, xs = slots
            bank = psum.tile([P, SS], F32, name="bank%d" % s)
            for i in range(SS // C):
                cols = slice(i * C, (i + 1) * C)
                nc.tensor.matmul_mx(
                    out=bank[:, cols],
                    lhsT=wc[:, cols].bitcast(FP8X4),
                    lhsT_scale=ws[:, cols],
                    rhs=xc[:, cols].bitcast(FP8X4),
                    rhs_scale=xs[:, cols],
                    start=True,
                    stop=True,
                )
            banks.append(bank)

        def take_out(s, tag):
            y = keep.tile([P, SS], F32, name="y%d" % s, tag=tag, align_bytes=64)
            if s < 2:
                nc.scalar.activation(out=y[:], in_=banks[s][:], func=COPY, scale=ones[s][:, 0:1])
            else:
                nc.scalar.copy(out=y[:], in_=banks[s][:])
            ys.append(y)

        def scatter(s):
            nc.vector.tensor_copy(
                out=result[:].indirect(offsets[:, s * SS // 16 : (s + 1) * SS // 16]), in_=ys[s][:]
            )

        wgs = [keep.tile([P, SS // C, N, 4], BF16, name="wg%d" % s, align_bytes=64) for s in range(2)]
        xgs = []
        for s in range(2):
            interleave_w(s, wgs[0])
            xg = keep.tile([P, SS, 2], U32, name="xg%d" % s, tag="wraw%d" % s, align_bytes=64)
            interleave_x(s, xg[:])
            xgs.append(xg)
        for g in range(2, 4):
            interleave_w(g, wgs[1])
        for s in range(2):
            weights = quantize("w%d" % s, wgs[s][:].rearrange("p e n j -> p (e n j)"))[0]
            slots = quantize("x%d" % s, xgs[s][:].rearrange("p n u -> p (n u)").bitcast(BF16))[0]
            multiply(s, weights, slots)
            if s == 0:
                gather(1, 3)
        for s in range(2, n_slices):
            take_out(s - 2, "wraw%d" % (2 * s - 1))
            scatter(s - 2)
            both = keep.tile([P, 2, 4 * SS], BF16, name="both%d" % s, tag="behind%d" % (s - 2), align_bytes=64)
            interleave_x(s, both[:, 1, :].bitcast(U32).rearrange("p (n u) -> p n u", u=2))
            wg = both[:, 0, :].rearrange("p (e n j) -> p e n j", n=N, j=4)
            for g in range(s * per, (s + 1) * per):
                interleave_w(g, wg)
            multiply(s, *quantize("both%d" % s, both[:].rearrange("p h c -> p (h c)")))
        for s in range(2, n_slices):
            take_out(s, "y%d" % s)
            scatter(s)

        nc.sync.dma_start(out=out, in_=result[:])
